import numpy as np
import ml_dtypes


def mxq(x, axis, fmt="e4m3"):
    dtype, down = {"e4m3": (ml_dtypes.float8_e4m3fn, 7), "e5m2": (ml_dtypes.float8_e5m2, 14)}[fmt]
    v = np.moveaxis(np.asarray(x, np.float32).astype(ml_dtypes.bfloat16).astype(np.float64), axis, -1)
    blocks = v.reshape(v.shape[:-1] + (-1, 32))
    amax = np.abs(blocks).max(-1, keepdims=True)
    byte = np.maximum(np.where(amax > 0, np.frexp(amax)[1] - 1 + 127, 0) - down, 1)
    scale = np.exp2(byte - 127.0)
    codes = (blocks / scale).astype(np.float32).astype(dtype).astype(np.float64)
    return np.moveaxis((codes * scale).reshape(v.shape), -1, axis)


WIDE = False


def mx_kscale(k):
    if not WIDE:
        return np.ones(k)
    levels = np.array([24, -24, 12, -12, 0])
    if k % 512:
        return np.exp2(np.random.permutation(np.resize(levels, k // 32))).repeat(32)
    a = np.empty((k // 512, 16))
    for p in range(k // 512):
        a[p, :8] = np.random.permutation(np.resize(levels, 8))
        for g in range(8):
            far = levels[np.abs(levels - a[p, g]) >= 10]
            a[p, g + 8] = far[np.random.randint(len(far))]
    return np.exp2(a.ravel()).repeat(32)


def f64(x):
    return np.asarray(x).astype(np.float64)


def striped8(idx):
    return np.concatenate([v.reshape(-1, 16).T for v in idx]).astype(np.uint16)


def unstriped8(offs):
    return np.stack([offs[16 * g:16 * g + 16].T.reshape(-1) for g in range(8)]).astype(np.int64)


E2M1 = np.array([0.0, 0.5, 1.0, 1.5, 2.0, 3.0, 4.0, 6.0, -0.0, -0.5, -1.0, -1.5, -2.0, -3.0, -4.0, -6.0])


def pack_weight(w, fmt):
    k, n = w.shape
    w = f64(np.asarray(w, np.float32).astype(ml_dtypes.bfloat16)).reshape(k // 32, 32, n)
    amax = np.abs(w).max(1)
    if fmt == "e4m3":
        byte = np.frexp(amax)[1] - 1 + 127 - 7
    else:
        mant, ex = np.frexp(amax / 6.0)
        byte = np.where(mant > 0.5, ex, ex - 1) + 127
    byte = np.clip(np.where(amax > 0, byte, 1), 1, 254)
    scaled = (w * np.exp2(127.0 - byte)[:, None, :]).reshape(k, n).astype(np.float32)
    by_word = np.ascontiguousarray(scaled.reshape(k // 512, 128, 4, n).transpose(0, 1, 3, 2))
    if fmt == "e4m3":
        words = by_word.astype(ml_dtypes.float8_e4m3fn).view(np.uint8)
    else:
        c = by_word.astype(ml_dtypes.float4_e2m1fn).view(np.uint8) & 0xF
        words = (c[..., 0::2] | (c[..., 1::2] << 4)).reshape(k // 512, 128, 2 * n)
    return np.ascontiguousarray(words), np.ascontiguousarray(byte.astype(np.uint8).reshape(k // 512, 16, n))


def unpack_weight(words, scales, fmt):
    g, _, n = scales.shape
    words = np.ascontiguousarray(words).reshape(g, 128, n, -1)
    if fmt == "e4m3":
        vals = words.view(ml_dtypes.float8_e4m3fn).astype(np.float64)
    else:
        nib = np.empty((g, 128, n, 4), np.uint8)
        nib[..., 0::2] = words & 0xF
        nib[..., 1::2] = words >> 4
        vals = E2M1[nib]
    vals = vals * np.repeat(np.exp2(scales.astype(np.float64) - 127.0), 8, axis=1)[..., None]
    return vals.transpose(0, 1, 3, 2).reshape(g * 512, n)


def planes(y):
    n, m = y.shape
    v = y.astype(np.float32).astype(ml_dtypes.bfloat16).astype(np.float64).reshape(n // 32, 32, m)
    top = np.abs(v).max(1)
    byte = np.clip(np.where(top > 0, np.frexp(top)[1] - 1 + 127 - 7, 1), 1, 254)
    codes = (v * np.exp2(127.0 - byte)[:, None, :]).reshape(n, m).astype(np.float32).astype(ml_dtypes.float8_e4m3fn).view(np.uint8)
    words = codes.reshape(n // 512, 128, 4, m).transpose(0, 1, 3, 2)
    return np.ascontiguousarray(words), np.ascontiguousarray(byte.astype(np.uint8).reshape(n // 512, 16, m))


def sigm(f):
    return 1.0 / (1.0 + np.exp(-np.maximum(f, -700.0)))


K, N, T, J = 512, 512, 2048, 1024


def setup_inputs():
    n = np.random.standard_normal
    s = mx_kscale(K)[:, None]
    p_wk = pack_weight(n((K, N)) / np.sqrt(K) / s, "e2m1")
    p_wv = pack_weight(n((K, N)) / np.sqrt(K) / s, "e2m1")
    return {
        "xT": (n((K, T)) * s).astype(np.float32),
        "wgt": np.repeat(np.random.uniform(0.5, 2.0, (8, J)), 16, axis=0).astype(np.float32),
        "wk_words": p_wk[0],
        "wk_scales": p_wk[1],
        "wv_words": p_wv[0],
        "wv_scales": p_wv[1],
        "bg": (0.3 * n(N) - 1.0).astype(np.float32),
        "res": (n((N, J))).astype(np.float32),
        "offs": striped8(np.stack([np.random.permutation(T)[:J] for _ in range(8)])),
    }


def reference(xT, wgt, wk_words, wk_scales, wv_words, wv_scales, bg, res, offs):
    idx = unstriped8(offs)
    rows = np.arange(K)
    xg = f64(wgt)[rows // 4 % 128] * f64(xT)[rows[:, None], idx[rows % 512 // 64]]
    xT_ = mxq(xg, 0, "e4m3")
    wk_ = unpack_weight(wk_words, wk_scales, "e2m1")
    wv_ = unpack_weight(wv_words, wv_scales, "e2m1")
    ke = wk_.T @ xT_
    ve = wv_.T @ xT_
    gate = sigm(ke + f64(bg)[:, None])
    out_0 = f64(res) + gate * (ve - f64(res))
    return (out_0,) + planes(out_0)

@@ -1,0 +1,169 @@
+from contextlib import ExitStack
+
+import concourse.mybir as mybir
+
+K, N, T, J = 512, 512, 2048, 1024
+FLOPS = 2 * 2 * K * N * J
+
+F32 = mybir.dt.float32
+BF16 = mybir.dt.bfloat16
+I32 = mybir.dt.int32
+U32 = mybir.dt.uint32
+U16 = mybir.dt.uint16
+U8 = mybir.dt.uint8
+FP8X4 = mybir.dt.float8_e4m3fn_x4
+FP4X4 = mybir.dt.float4_e2m1fn_x4
+ALU = mybir.AluOpType
+ACT = mybir.ActivationFunctionType
+
+P = 128
+PACK = 4
+BANK = 512
+LIST_ROWS = 16
+CHUNKS = (256, 256, 256, 256)
+
+
+def interleave(engine_copy, dst, src):
+    engine_copy(
+        out=dst.rearrange("p (c i) t -> p c t i", i=4),
+        in_=src.rearrange("p t (c i) -> p c t i", i=4),
+    )
+
+
+def tile_list_hwayP_kernel(
+    tc, xT, wgt, wk_words, wk_scales, wv_words, wv_scales, bg, res, offs, out_0, out_1, out_2
+):
+    nc = tc.nc
+    starts = [sum(CHUNKS[:c]) for c in range(len(CHUNKS))]
+    half = J // 2
+    x_rows = xT.rearrange("(p i) t -> p i t", i=PACK)
+    res_rows = res.rearrange("(p t) j -> p t j", t=PACK)
+    out_rows = out_0.rearrange("(p t) j -> p t j", t=PACK)
+    out_words = out_1[0].rearrange("p j i -> p (j i)").bitcast(I32)
+
+    with ExitStack() as ctx:
+        keep = ctx.enter_context(tc.tile_pool(name="keep", bufs=1))
+        psum = ctx.enter_context(tc.psum_pool(name="psum", bufs=2))
+
+        offsets = keep.tile([P, J // LIST_ROWS], U16, name="offsets")
+        nc.sync.dma_start(offsets[:], offs)
+
+        raw_scales = [keep.tile([P, N], U8, name=f"raw_scales{w}") for w in range(2)]
+        for w in range(2):
+            nc.gpsimd.memset(raw_scales[w][:].bitcast(I32), 0)
+        for q in range(4):
+            nc.scalar.dma_start(
+                raw_scales[0][32 * q : 32 * q + 4, :].bitcast(I32), wk_scales[0, 4 * q : 4 * q + 4, :].bitcast(I32)
+            )
+        for q in range(4):
+            nc.gpsimd.dma_start(
+                raw_scales[1][32 * q : 32 * q + 4, :].bitcast(I32), wv_scales[0, 4 * q : 4 * q + 4, :].bitcast(I32)
+            )
+        bias = keep.tile([P, PACK], F32, name="bias")
+        nc.gpsimd.dma_start(bias[:], bg.rearrange("(p t) -> p t", t=PACK))
+
+        raw_words = [keep.tile([P, 2 * N], U8, name=f"raw_words{w}") for w in range(2)]
+        for w, words in enumerate((wk_words, wv_words)):
+            nc.sync.dma_start(raw_words[w][:].bitcast(I32), words[0].bitcast(I32))
+
+        planes = [keep.tile([P, T], F32, name=f"plane{i}") for i in range(PACK)]
+        weight = keep.tile([P, J], F32, name="weight")
+        nc.sync.dma_start(planes[0][:], x_rows[:, 0, :])
+        nc.sync.dma_start(weight[:, :half], wgt[:, :half])
+        nc.sync.dma_start(weight[:, half:], wgt[:, half:])
+        for i in range(1, PACK):
+            nc.sync.dma_start(planes[i][:], x_rows[:, i, :])
+        carried = []
+        for c, (j0, width) in enumerate(zip(starts, CHUNKS)):
+            res_c = keep.tile([P, PACK, width], F32, name=f"res{c}")
+            nc.sync.dma_start(res_c[:], res_rows[:, :, j0 : j0 + width])
+            carried.append(res_c)
+
+        warm_in = keep.tile([P, 1], F32, name="warm_in")
+        warm_out = keep.tile([P, 1], F32, name="warm_out")
+        nc.vector.memset(warm_in[:], 0.0)
+        nc.scalar.activation(warm_out[:], warm_in[:], ACT.Sigmoid)
+
+        w_words = [keep.tile([P, PACK, 2 * P], U8, name=f"w_words{w}", align_bytes=64) for w in range(2)]
+        w_scales = [keep.tile([P, PACK, P], U8, name=f"w_scales{w}", align_bytes=64) for w in range(2)]
+        for w in range(2):
+            nc.vector.tensor_copy(
+                w_words[w][:].rearrange("p t (m b) -> p t m b", b=2),
+                raw_words[w][:].rearrange("p (m t b) -> p t m b", t=PACK, b=2),
+            )
+        for w in range(2):
+            nc.vector.tensor_copy(w_scales[w][:], raw_scales[w][:].rearrange("p (m t) -> p t m", t=PACK))
+
+        picked = keep.tile([P, PACK, J], F32, name="picked")
+
+        def gather(i, j0, width):
+            listed = offsets[:, j0 // LIST_ROWS : (j0 + width) // LIST_ROWS]
+            nc.vector.tensor_tensor(
+                picked[:, i, j0 : j0 + width], planes[i][:].indirect(listed), weight[:, j0 : j0 + width], ALU.mult
+            )
+
+        gather(0, 0, half)
+        gather(0, half, half)
+        gather(1, 0, J)
+        gather(2, 0, J)
+
+        y_scales = keep.tile([P, J], U8, name="y_scales", align_bytes=64)
+        x_codes, x_scales = [], []
+        for c, (j0, width) in enumerate(zip(starts, CHUNKS)):
+            gather(PACK - 1, j0, width)
+            x_bf = keep.tile([P, width, PACK], BF16, name=f"x_bf{c}", align_bytes=64)
+            interleave(nc.scalar.copy, x_bf[:], picked[:, :, j0 : j0 + width])
+            codes = keep.tile([P, width], U32, name=f"x_codes{c}", align_bytes=64)
+            scales = keep.tile([P, width], U8, name=f"x_scales{c}", align_bytes=64)
+            nc.vector.quantize_mx(
+                out=codes[:].bitcast(FP8X4), scales=scales[:], in_=x_bf[:].rearrange("p j t -> p (j t)")
+            )
+            x_codes.append(codes)
+            x_scales.append(scales)
+
+        for c, (j0, width) in enumerate(zip(starts, CHUNKS)):
+            per_bank = min(PACK, BANK // width)
+            groups = [range(t0, t0 + per_bank) for t0 in range(0, PACK, per_bank)]
+            gate = keep.tile([P, PACK, width], F32, name=f"gate{c}")
+            diff = keep.tile([P, PACK, width], F32, name=f"diff{c}")
+            gated = keep.tile([P, PACK, width], F32, name=f"gated{c}")
+            y = keep.tile([P, PACK, width], F32, name=f"y{c}")
+            for g, slices in enumerate(groups):
+                rows = slice(slices.start, slices.stop)
+                ve = psum.tile([P, per_bank, width], F32, name=f"ve{g}")
+                ke = psum.tile([P, per_bank, width], F32, name=f"ke{g}")
+                for w, bank in ((1, ve), (0, ke)):
+                    for t in slices:
+                        nc.tensor.matmul_mx(
+                            out=bank[:, t - slices.start, :],
+                            lhsT=w_words[w][:, t, :].bitcast(FP4X4),
+                            lhsT_scale=w_scales[w][:, t, :],
+                            rhs=x_codes[c][:].bitcast(FP8X4),
+                            rhs_scale=x_scales[c][:],
+                            start=True,
+                            stop=True,
+                        )
+                for t in slices:
+                    nc.scalar.activation(
+                        gate[:, t, :], ke[:, t - slices.start, :], ACT.Sigmoid, bias=bias[:, t : t + 1]
+                    )
+                nc.vector.tensor_tensor(diff[:, rows, :], ve[:], carried[c][:, rows, :], ALU.subtract)
+            for slices in groups:
+                rows = slice(slices.start, slices.stop)
+                nc.vector.tensor_tensor(gated[:, rows, :], diff[:, rows, :], gate[:, rows, :], ALU.mult)
+            for slices in groups:
+                rows = slice(slices.start, slices.stop)
+                nc.vector.tensor_tensor(y[:, rows, :], gated[:, rows, :], carried[c][:, rows, :], ALU.add)
+            nc.sync.dma_start(out_rows[:, :, j0 : j0 + width], y[:])
+            y_bf = keep.tile([P, width, PACK], BF16, name=f"y_bf{c}", align_bytes=64)
+            interleave(nc.scalar.copy, y_bf[:], y[:])
+            y_codes = keep.tile([P, width], U32, name=f"y_codes{c}", align_bytes=64)
+            nc.vector.quantize_mx(
+                out=y_codes[:].bitcast(FP8X4),
+                scales=y_scales[:, j0 : j0 + width],
+                in_=y_bf[:].rearrange("p j t -> p (j t)"),
+            )
+            nc.sync.dma_start(out_words[:, j0 : j0 + width], y_codes[:].bitcast(I32))
+        for q in range(4):
+            queue = nc.sync if q % 2 == 0 else nc.scalar
+            queue.dma_start(out_2[0, 4 * q : 4 * q + 4, :].bitcast(I32), y_scales[32 * q : 32 * q + 4, :].bitcast(I32))

@@ -20,7 +20,7 @@ P = 128
 PACK = 4
 BANK = 512
 LIST_ROWS = 16
-CHUNKS = (256, 256, 256, 256)
+CHUNKS = (128, 256, 256, 256, 128)
 
 
 def interleave(engine_copy, dst, src):
@@ -35,7 +35,7 @@ def tile_list_hwayP_kernel(
 ):
     nc = tc.nc
     starts = [sum(CHUNKS[:c]) for c in range(len(CHUNKS))]
-    half = J // 2
+    half = starts[2]
     x_rows = xT.rearrange("(p i) t -> p i t", i=PACK)
     res_rows = res.rearrange("(p t) j -> p t j", t=PACK)
     out_rows = out_0.rearrange("(p t) j -> p t j", t=PACK)
@@ -51,16 +51,14 @@ def tile_list_hwayP_kernel(
         raw_scales = [keep.tile([P, N], U8, name=f"raw_scales{w}") for w in range(2)]
         for w in range(2):
             nc.gpsimd.memset(raw_scales[w][:].bitcast(I32), 0)
-        for q in range(4):
-            nc.scalar.dma_start(
-                raw_scales[0][32 * q : 32 * q + 4, :].bitcast(I32), wk_scales[0, 4 * q : 4 * q + 4, :].bitcast(I32)
-            )
-        for q in range(4):
-            nc.gpsimd.dma_start(
-                raw_scales[1][32 * q : 32 * q + 4, :].bitcast(I32), wv_scales[0, 4 * q : 4 * q + 4, :].bitcast(I32)
-            )
+        for w, scale_rows in enumerate((wk_scales, wv_scales)):
+            for q in range(4):
+                nc.scalar.dma_start(
+                    raw_scales[w][32 * q : 32 * q + 4, :].bitcast(I32),
+                    scale_rows[0, 4 * q : 4 * q + 4, :].bitcast(I32),
+                )
         bias = keep.tile([P, PACK], F32, name="bias")
-        nc.gpsimd.dma_start(bias[:], bg.rearrange("(p t) -> p t", t=PACK))
+        nc.scalar.dma_start(bias[:], bg.rearrange("(p t) -> p t", t=PACK))
 
         raw_words = [keep.tile([P, 2 * N], U8, name=f"raw_words{w}") for w in range(2)]
         for w, words in enumerate((wk_words, wv_words)):
@@ -81,7 +79,7 @@ def tile_list_hwayP_kernel(
 
         warm_in = keep.tile([P, 1], F32, name="warm_in")
         warm_out = keep.tile([P, 1], F32, name="warm_out")
-        nc.vector.memset(warm_in[:], 0.0)
+        nc.gpsimd.memset(warm_in[:], 0.0)
         nc.scalar.activation(warm_out[:], warm_in[:], ACT.Sigmoid)
 
         w_words = [keep.tile([P, PACK, 2 * P], U8, name=f"w_words{w}", align_bytes=64) for w in range(2)]
@@ -94,25 +92,23 @@ def tile_list_hwayP_kernel(
         for w in range(2):
             nc.vector.tensor_copy(w_scales[w][:], raw_scales[w][:].rearrange("p (m t) -> p t m", t=PACK))
 
-        picked = keep.tile([P, PACK, J], F32, name="picked")
+        picked = [keep.tile([P, PACK, width], F32, name=f"picked{c}") for c, width in enumerate(CHUNKS)]
 
-        def gather(i, j0, width):
-            listed = offsets[:, j0 // LIST_ROWS : (j0 + width) // LIST_ROWS]
-            nc.vector.tensor_tensor(
-                picked[:, i, j0 : j0 + width], planes[i][:].indirect(listed), weight[:, j0 : j0 + width], ALU.mult
-            )
+        def gather(i, c):
+            j0, j1 = starts[c], starts[c] + CHUNKS[c]
+            listed = offsets[:, j0 // LIST_ROWS : j1 // LIST_ROWS]
+            nc.vector.tensor_tensor(picked[c][:, i, :], planes[i][:].indirect(listed), weight[:, j0:j1], ALU.mult)
 
-        gather(0, 0, half)
-        gather(0, half, half)
-        gather(1, 0, J)
-        gather(2, 0, J)
+        for i in range(PACK - 1):
+            for c in range(len(CHUNKS)):
+                gather(i, c)
 
         y_scales = keep.tile([P, J], U8, name="y_scales", align_bytes=64)
         x_codes, x_scales = [], []
         for c, (j0, width) in enumerate(zip(starts, CHUNKS)):
-            gather(PACK - 1, j0, width)
+            gather(PACK - 1, c)
             x_bf = keep.tile([P, width, PACK], BF16, name=f"x_bf{c}", align_bytes=64)
-            interleave(nc.scalar.copy, x_bf[:], picked[:, :, j0 : j0 + width])
+            interleave(nc.scalar.copy, x_bf[:], picked[c][:])
             codes = keep.tile([P, width], U32, name=f"x_codes{c}", align_bytes=64)
             scales = keep.tile([P, width], U8, name=f"x_scales{c}", align_bytes=64)
             nc.vector.quantize_mx(
@@ -122,7 +118,7 @@ def tile_list_hwayP_kernel(
             x_scales.append(scales)
 
         for c, (j0, width) in enumerate(zip(starts, CHUNKS)):
-            per_bank = min(PACK, BANK // width)
+            per_bank = 2
             groups = [range(t0, t0 + per_bank) for t0 in range(0, PACK, per_bank)]
             gate = keep.tile([P, PACK, width], F32, name=f"gate{c}")
             diff = keep.tile([P, PACK, width], F32, name=f"diff{c}")
@@ -156,7 +152,8 @@ def tile_list_hwayP_kernel(
                 nc.vector.tensor_tensor(y[:, rows, :], gated[:, rows, :], carried[c][:, rows, :], ALU.add)
             nc.sync.dma_start(out_rows[:, :, j0 : j0 + width], y[:])
             y_bf = keep.tile([P, width, PACK], BF16, name=f"y_bf{c}", align_bytes=64)
-            interleave(nc.scalar.copy, y_bf[:], y[:])
+            last = c == len(CHUNKS) - 1
+            interleave(nc.vector.tensor_copy if last else nc.scalar.copy, y_bf[:], y[:])
             y_codes = keep.tile([P, width], U32, name=f"y_codes{c}", align_bytes=64)
             nc.vector.quantize_mx(
                 out=y_codes[:].bitcast(FP8X4),

@@ -18,7 +18,8 @@ ACT = mybir.ActivationFunctionType
 
 P = 128
 PACK = 4
-BANK = 512
+GROUP = 2
+VECTOR_GROUPS = 3
 LIST_ROWS = 16
 CHUNKS = (128, 256, 256, 256, 128)
 
@@ -43,44 +44,44 @@ def tile_list_hwayP_kernel(
 
     with ExitStack() as ctx:
         keep = ctx.enter_context(tc.tile_pool(name="keep", bufs=1))
-        psum = ctx.enter_context(tc.psum_pool(name="psum", bufs=2))
+        ve_banks = ctx.enter_context(tc.psum_pool(name="ve_banks", bufs=3))
+        ke_banks = ctx.enter_context(tc.psum_pool(name="ke_banks", bufs=1))
 
         offsets = keep.tile([P, J // LIST_ROWS], U16, name="offsets")
-        nc.sync.dma_start(offsets[:], offs)
-
         raw_scales = [keep.tile([P, N], U8, name=f"raw_scales{w}") for w in range(2)]
+        raw_words = [keep.tile([P, 2 * N], U8, name=f"raw_words{w}") for w in range(2)]
+        planes = [keep.tile([P, T], F32, name=f"plane{i}") for i in range(PACK)]
+        weight = keep.tile([P, J], F32, name="weight")
+        bias = keep.tile([P, PACK], F32, name="bias")
         for w in range(2):
             nc.gpsimd.memset(raw_scales[w][:].bitcast(I32), 0)
-        for w, scale_rows in enumerate((wk_scales, wv_scales)):
+
+        def load_scales(w, scale_rows):
             for q in range(4):
-                nc.scalar.dma_start(
+                nc.sync.dma_start(
                     raw_scales[w][32 * q : 32 * q + 4, :].bitcast(I32),
                     scale_rows[0, 4 * q : 4 * q + 4, :].bitcast(I32),
                 )
-        bias = keep.tile([P, PACK], F32, name="bias")
-        nc.scalar.dma_start(bias[:], bg.rearrange("(p t) -> p t", t=PACK))
 
-        raw_words = [keep.tile([P, 2 * N], U8, name=f"raw_words{w}") for w in range(2)]
         for w, words in enumerate((wk_words, wv_words)):
             nc.sync.dma_start(raw_words[w][:].bitcast(I32), words[0].bitcast(I32))
-
-        planes = [keep.tile([P, T], F32, name=f"plane{i}") for i in range(PACK)]
-        weight = keep.tile([P, J], F32, name="weight")
+        nc.sync.dma_start(offsets[:], offs)
         nc.sync.dma_start(planes[0][:], x_rows[:, 0, :])
+        load_scales(0, wk_scales)
         nc.sync.dma_start(weight[:, :half], wgt[:, :half])
         nc.sync.dma_start(weight[:, half:], wgt[:, half:])
-        for i in range(1, PACK):
+        nc.sync.dma_start(planes[1][:], x_rows[:, 1, :])
+        load_scales(1, wv_scales)
+        for i in range(2, PACK):
             nc.sync.dma_start(planes[i][:], x_rows[:, i, :])
+        nc.sync.dma_start(bias[:], bg.rearrange("(p t) -> p t", t=PACK))
+        neg_bias = keep.tile([P, PACK], F32, name="neg_bias")
+        nc.scalar.mul(neg_bias[:], bias[:], -1.0)
         carried = []
         for c, (j0, width) in enumerate(zip(starts, CHUNKS)):
             res_c = keep.tile([P, PACK, width], F32, name=f"res{c}")
             nc.sync.dma_start(res_c[:], res_rows[:, :, j0 : j0 + width])
             carried.append(res_c)
-
-        warm_in = keep.tile([P, 1], F32, name="warm_in")
-        warm_out = keep.tile([P, 1], F32, name="warm_out")
-        nc.gpsimd.memset(warm_in[:], 0.0)
-        nc.scalar.activation(warm_out[:], warm_in[:], ACT.Sigmoid)
 
         w_words = [keep.tile([P, PACK, 2 * P], U8, name=f"w_words{w}", align_bytes=64) for w in range(2)]
         w_scales = [keep.tile([P, PACK, P], U8, name=f"w_scales{w}", align_bytes=64) for w in range(2)]
@@ -92,64 +93,83 @@ def tile_list_hwayP_kernel(
         for w in range(2):
             nc.vector.tensor_copy(w_scales[w][:], raw_scales[w][:].rearrange("p (m t) -> p t m", t=PACK))
 
-        picked = [keep.tile([P, PACK, width], F32, name=f"picked{c}") for c, width in enumerate(CHUNKS)]
+        picked_row = keep.tile([P, PACK * J], F32, name="picked_row")
+        picked = picked_row[:].rearrange("p (i j) -> p i j", i=PACK)
 
-        def gather(i, c):
-            j0, j1 = starts[c], starts[c] + CHUNKS[c]
+        def gather(i, j0, j1):
             listed = offsets[:, j0 // LIST_ROWS : j1 // LIST_ROWS]
-            nc.vector.tensor_tensor(picked[c][:, i, :], planes[i][:].indirect(listed), weight[:, j0:j1], ALU.mult)
+            nc.vector.tensor_tensor(
+                picked_row[:, i * J + j0 : i * J + j1], planes[i][:].indirect(listed), weight[:, j0:j1], ALU.mult
+            )
 
-        for i in range(PACK - 1):
-            for c in range(len(CHUNKS)):
-                gather(i, c)
+        gather(0, 0, half)
+        gather(0, half, J)
+        gather(1, 0, J)
+        x_bf = [keep.tile([P, width, PACK], BF16, name=f"x_bf{c}", align_bytes=64) for c, width in enumerate(CHUNKS)]
+
+        def round_pair(i, c):
+            j0, j1 = starts[c], starts[c] + CHUNKS[c]
+            nc.scalar.copy(x_bf[c][:, :, i : i + 2], picked[:, i : i + 2, j0:j1].rearrange("p t j -> p j t"))
+
+        for c in range(len(CHUNKS)):
+            round_pair(0, c)
+        gather(2, 0, J)
 
         y_scales = keep.tile([P, J], U8, name="y_scales", align_bytes=64)
-        x_codes, x_scales = [], []
-        for c, (j0, width) in enumerate(zip(starts, CHUNKS)):
-            gather(PACK - 1, c)
-            x_bf = keep.tile([P, width, PACK], BF16, name=f"x_bf{c}", align_bytes=64)
-            interleave(nc.scalar.copy, x_bf[:], picked[c][:])
+        groups = [range(t0, t0 + GROUP) for t0 in range(0, PACK, GROUP)]
+        quantised, multiplied = {}, {}
+
+        def front(c):
+            j0, width = starts[c], CHUNKS[c]
+            gather(PACK - 1, j0, j0 + width)
+            round_pair(2, c)
             codes = keep.tile([P, width], U32, name=f"x_codes{c}", align_bytes=64)
             scales = keep.tile([P, width], U8, name=f"x_scales{c}", align_bytes=64)
             nc.vector.quantize_mx(
-                out=codes[:].bitcast(FP8X4), scales=scales[:], in_=x_bf[:].rearrange("p j t -> p (j t)")
+                out=codes[:].bitcast(FP8X4), scales=scales[:], in_=x_bf[c][:].rearrange("p j t -> p (j t)")
             )
-            x_codes.append(codes)
-            x_scales.append(scales)
+            quantised[c] = (codes, scales)
 
-        for c, (j0, width) in enumerate(zip(starts, CHUNKS)):
-            per_bank = 2
-            groups = [range(t0, t0 + per_bank) for t0 in range(0, PACK, per_bank)]
+        def products(c):
+            width = CHUNKS[c]
+            codes, scales = quantised[c]
             gate = keep.tile([P, PACK, width], F32, name=f"gate{c}")
             diff = keep.tile([P, PACK, width], F32, name=f"diff{c}")
             gated = keep.tile([P, PACK, width], F32, name=f"gated{c}")
-            y = keep.tile([P, PACK, width], F32, name=f"y{c}")
+            values = []
             for g, slices in enumerate(groups):
                 rows = slice(slices.start, slices.stop)
-                ve = psum.tile([P, per_bank, width], F32, name=f"ve{g}")
-                ke = psum.tile([P, per_bank, width], F32, name=f"ke{g}")
-                for w, bank in ((1, ve), (0, ke)):
+                ve = ve_banks.tile([P, GROUP, width], F32, name=f"ve{g}")
+                ke = ke_banks.tile([P, GROUP, width], F32, name=f"ke{g}")
+                for w, bank in ((0, ke), (1, ve)):
                     for t in slices:
                         nc.tensor.matmul_mx(
                             out=bank[:, t - slices.start, :],
                             lhsT=w_words[w][:, t, :].bitcast(FP4X4),
                             lhsT_scale=w_scales[w][:, t, :],
-                            rhs=x_codes[c][:].bitcast(FP8X4),
-                            rhs_scale=x_scales[c][:],
+                            rhs=codes[:].bitcast(FP8X4),
+                            rhs_scale=scales[:],
                             start=True,
                             stop=True,
                         )
                 for t in slices:
                     nc.scalar.activation(
-                        gate[:, t, :], ke[:, t - slices.start, :], ACT.Sigmoid, bias=bias[:, t : t + 1]
+                        gate[:, t, :], ke[:, t - slices.start, :], ACT.Sigmoid, bias=neg_bias[:, t : t + 1], scale=-1.0
                     )
                 nc.vector.tensor_tensor(diff[:, rows, :], ve[:], carried[c][:, rows, :], ALU.subtract)
-            for slices in groups:
+                from_end = (len(CHUNKS) - c) * len(groups) - g
+                engine = nc.vector if from_end <= VECTOR_GROUPS else nc.gpsimd
+                engine.tensor_tensor(gated[:, rows, :], diff[:, rows, :], gate[:, rows, :], ALU.mult)
+                values.append(ve)
+            multiplied[c] = (values, gated)
+
+        def finish(c):
+            j0, width = starts[c], CHUNKS[c]
+            values, gated = multiplied[c]
+            y = keep.tile([P, PACK, width], F32, name=f"y{c}")
+            for ve, slices in zip(values, groups):
                 rows = slice(slices.start, slices.stop)
-                nc.vector.tensor_tensor(gated[:, rows, :], diff[:, rows, :], gate[:, rows, :], ALU.mult)
-            for slices in groups:
-                rows = slice(slices.start, slices.stop)
-                nc.vector.tensor_tensor(y[:, rows, :], gated[:, rows, :], carried[c][:, rows, :], ALU.add)
+                nc.vector.tensor_tensor(y[:, rows, :], ve[:], gated[:, rows, :], ALU.subtract)
             nc.sync.dma_start(out_rows[:, :, j0 : j0 + width], y[:])
             y_bf = keep.tile([P, width, PACK], BF16, name=f"y_bf{c}", align_bytes=64)
             last = c == len(CHUNKS) - 1
@@ -161,6 +181,11 @@ def tile_list_hwayP_kernel(
                 in_=y_bf[:].rearrange("p j t -> p (j t)"),
             )
             nc.sync.dma_start(out_words[:, j0 : j0 + width], y_codes[:].bitcast(I32))
+
+        for step in range(len(CHUNKS) + 2):
+            for stage, c in ((front, step), (products, step - 1), (finish, step - 2)):
+                if 0 <= c < len(CHUNKS):
+                    stage(c)
         for q in range(4):
             queue = nc.sync if q % 2 == 0 else nc.scalar
             queue.dma_start(out_2[0, 4 * q : 4 * q + 4, :].bitcast(I32), y_scales[32 * q : 32 * q + 4, :].bitcast(I32))

@@ -56,6 +56,11 @@ def tile_list_hwayP_kernel(
         for w in range(2):
             nc.gpsimd.memset(raw_scales[w][:].bitcast(I32), 0)
 
+        warm_in = keep.tile([P, 1], F32, name="warm_in")
+        warm_out = keep.tile([P, 1], F32, name="warm_out")
+        nc.gpsimd.memset(warm_in[:], 0.0)
+        nc.scalar.activation(warm_out[:], warm_in[:], ACT.Sigmoid)
+
         def load_scales(w, scale_rows):
             for q in range(4):
                 nc.sync.dma_start(

from contextlib import ExitStack

import concourse.mybir as mybir

K, N, T, J = 512, 512, 2048, 1024
FLOPS = 2 * 2 * K * N * J

F32 = mybir.dt.float32
BF16 = mybir.dt.bfloat16
I32 = mybir.dt.int32
U32 = mybir.dt.uint32
U16 = mybir.dt.uint16
U8 = mybir.dt.uint8
FP8X4 = mybir.dt.float8_e4m3fn_x4
FP4X4 = mybir.dt.float4_e2m1fn_x4
ALU = mybir.AluOpType
ACT = mybir.ActivationFunctionType

P = 128
PACK = 4
GROUP = 2
VECTOR_GROUPS = 3
LIST_ROWS = 16
CHUNKS = (128, 256, 256, 256, 128)


def interleave(engine_copy, dst, src):
    engine_copy(
        out=dst.rearrange("p (c i) t -> p c t i", i=4),
        in_=src.rearrange("p t (c i) -> p c t i", i=4),
    )


def tile_list_hwayP_kernel(
    tc, xT, wgt, wk_words, wk_scales, wv_words, wv_scales, bg, res, offs, out_0, out_1, out_2
):
    nc = tc.nc
    starts = [sum(CHUNKS[:c]) for c in range(len(CHUNKS))]
    half = starts[2]
    x_rows = xT.rearrange("(p i) t -> p i t", i=PACK)
    res_rows = res.rearrange("(p t) j -> p t j", t=PACK)
    out_rows = out_0.rearrange("(p t) j -> p t j", t=PACK)
    out_words = out_1[0].rearrange("p j i -> p (j i)").bitcast(I32)

    with ExitStack() as ctx:
        keep = ctx.enter_context(tc.tile_pool(name="keep", bufs=1))
        ve_banks = ctx.enter_context(tc.psum_pool(name="ve_banks", bufs=3))
        ke_banks = ctx.enter_context(tc.psum_pool(name="ke_banks", bufs=1))

        offsets = keep.tile([P, J // LIST_ROWS], U16, name="offsets")
        raw_scales = [keep.tile([P, N], U8, name=f"raw_scales{w}") for w in range(2)]
        raw_words = [keep.tile([P, 2 * N], U8, name=f"raw_words{w}") for w in range(2)]
        planes = [keep.tile([P, T], F32, name=f"plane{i}") for i in range(PACK)]
        weight = keep.tile([P, J], F32, name="weight")
        bias = keep.tile([P, PACK], F32, name="bias")
        for w in range(2):
            nc.gpsimd.memset(raw_scales[w][:].bitcast(I32), 0)

        warm_in = keep.tile([P, 1], F32, name="warm_in")
        warm_out = keep.tile([P, 1], F32, name="warm_out")
        nc.gpsimd.memset(warm_in[:], 0.0)
        nc.scalar.activation(warm_out[:], warm_in[:], ACT.Sigmoid)

        def load_scales(w, scale_rows):
            for q in range(4):
                nc.sync.dma_start(
                    raw_scales[w][32 * q : 32 * q + 4, :].bitcast(I32),
                    scale_rows[0, 4 * q : 4 * q + 4, :].bitcast(I32),
                )

        for w, words in enumerate((wk_words, wv_words)):
            nc.sync.dma_start(raw_words[w][:].bitcast(I32), words[0].bitcast(I32))
        nc.sync.dma_start(offsets[:], offs)
        nc.sync.dma_start(planes[0][:], x_rows[:, 0, :])
        load_scales(0, wk_scales)
        nc.sync.dma_start(weight[:, :half], wgt[:, :half])
        nc.sync.dma_start(weight[:, half:], wgt[:, half:])
        nc.sync.dma_start(planes[1][:], x_rows[:, 1, :])
        load_scales(1, wv_scales)
        for i in range(2, PACK):
            nc.sync.dma_start(planes[i][:], x_rows[:, i, :])
        nc.sync.dma_start(bias[:], bg.rearrange("(p t) -> p t", t=PACK))
        neg_bias = keep.tile([P, PACK], F32, name="neg_bias")
        nc.scalar.mul(neg_bias[:], bias[:], -1.0)
        carried = []
        for c, (j0, width) in enumerate(zip(starts, CHUNKS)):
            res_c = keep.tile([P, PACK, width], F32, name=f"res{c}")
            nc.sync.dma_start(res_c[:], res_rows[:, :, j0 : j0 + width])
            carried.append(res_c)

        w_words = [keep.tile([P, PACK, 2 * P], U8, name=f"w_words{w}", align_bytes=64) for w in range(2)]
        w_scales = [keep.tile([P, PACK, P], U8, name=f"w_scales{w}", align_bytes=64) for w in range(2)]
        for w in range(2):
            nc.vector.tensor_copy(
                w_words[w][:].rearrange("p t (m b) -> p t m b", b=2),
                raw_words[w][:].rearrange("p (m t b) -> p t m b", t=PACK, b=2),
            )
        for w in range(2):
            nc.vector.tensor_copy(w_scales[w][:], raw_scales[w][:].rearrange("p (m t) -> p t m", t=PACK))

        picked_row = keep.tile([P, PACK * J], F32, name="picked_row")
        picked = picked_row[:].rearrange("p (i j) -> p i j", i=PACK)

        def gather(i, j0, j1):
            listed = offsets[:, j0 // LIST_ROWS : j1 // LIST_ROWS]
            nc.vector.tensor_tensor(
                picked_row[:, i * J + j0 : i * J + j1], planes[i][:].indirect(listed), weight[:, j0:j1], ALU.mult
            )

        gather(0, 0, half)
        gather(0, half, J)
        gather(1, 0, J)
        x_bf = [keep.tile([P, width, PACK], BF16, name=f"x_bf{c}", align_bytes=64) for c, width in enumerate(CHUNKS)]

        def round_pair(i, c):
            j0, j1 = starts[c], starts[c] + CHUNKS[c]
            nc.scalar.copy(x_bf[c][:, :, i : i + 2], picked[:, i : i + 2, j0:j1].rearrange("p t j -> p j t"))

        for c in range(len(CHUNKS)):
            round_pair(0, c)
        gather(2, 0, J)

        y_scales = keep.tile([P, J], U8, name="y_scales", align_bytes=64)
        groups = [range(t0, t0 + GROUP) for t0 in range(0, PACK, GROUP)]
        quantised, multiplied = {}, {}

        def front(c):
            j0, width = starts[c], CHUNKS[c]
            gather(PACK - 1, j0, j0 + width)
            round_pair(2, c)
            codes = keep.tile([P, width], U32, name=f"x_codes{c}", align_bytes=64)
            scales = keep.tile([P, width], U8, name=f"x_scales{c}", align_bytes=64)
            nc.vector.quantize_mx(
                out=codes[:].bitcast(FP8X4), scales=scales[:], in_=x_bf[c][:].rearrange("p j t -> p (j t)")
            )
            quantised[c] = (codes, scales)

        def products(c):
            width = CHUNKS[c]
            codes, scales = quantised[c]
            gate = keep.tile([P, PACK, width], F32, name=f"gate{c}")
            diff = keep.tile([P, PACK, width], F32, name=f"diff{c}")
            gated = keep.tile([P, PACK, width], F32, name=f"gated{c}")
            values = []
            for g, slices in enumerate(groups):
                rows = slice(slices.start, slices.stop)
                ve = ve_banks.tile([P, GROUP, width], F32, name=f"ve{g}")
                ke = ke_banks.tile([P, GROUP, width], F32, name=f"ke{g}")
                for w, bank in ((0, ke), (1, ve)):
                    for t in slices:
                        nc.tensor.matmul_mx(
                            out=bank[:, t - slices.start, :],
                            lhsT=w_words[w][:, t, :].bitcast(FP4X4),
                            lhsT_scale=w_scales[w][:, t, :],
                            rhs=codes[:].bitcast(FP8X4),
                            rhs_scale=scales[:],
                            start=True,
                            stop=True,
                        )
                for t in slices:
                    nc.scalar.activation(
                        gate[:, t, :], ke[:, t - slices.start, :], ACT.Sigmoid, bias=neg_bias[:, t : t + 1], scale=-1.0
                    )
                nc.vector.tensor_tensor(diff[:, rows, :], ve[:], carried[c][:, rows, :], ALU.subtract)
                from_end = (len(CHUNKS) - c) * len(groups) - g
                engine = nc.vector if from_end <= VECTOR_GROUPS else nc.gpsimd
                engine.tensor_tensor(gated[:, rows, :], diff[:, rows, :], gate[:, rows, :], ALU.mult)
                values.append(ve)
            multiplied[c] = (values, gated)

        def finish(c):
            j0, width = starts[c], CHUNKS[c]
            values, gated = multiplied[c]
            y = keep.tile([P, PACK, width], F32, name=f"y{c}")
            for ve, slices in zip(values, groups):
                rows = slice(slices.start, slices.stop)
                nc.vector.tensor_tensor(y[:, rows, :], ve[:], gated[:, rows, :], ALU.subtract)
            nc.sync.dma_start(out_rows[:, :, j0 : j0 + width], y[:])
            y_bf = keep.tile([P, width, PACK], BF16, name=f"y_bf{c}", align_bytes=64)
            last = c == len(CHUNKS) - 1
            interleave(nc.vector.tensor_copy if last else nc.scalar.copy, y_bf[:], y[:])
            y_codes = keep.tile([P, width], U32, name=f"y_codes{c}", align_bytes=64)
            nc.vector.quantize_mx(
                out=y_codes[:].bitcast(FP8X4),
                scales=y_scales[:, j0 : j0 + width],
                in_=y_bf[:].rearrange("p j t -> p (j t)"),
            )
            nc.sync.dma_start(out_words[:, j0 : j0 + width], y_codes[:].bitcast(I32))

        for step in range(len(CHUNKS) + 2):
            for stage, c in ((front, step), (products, step - 1), (finish, step - 2)):
                if 0 <= c < len(CHUNKS):
                    stage(c)
        for q in range(4):
            queue = nc.sync if q % 2 == 0 else nc.scalar
            queue.dma_start(out_2[0, 4 * q : 4 * q + 4, :].bitcast(I32), y_scales[32 * q : 32 * q + 4, :].bitcast(I32))
